import numpy as np
import ml_dtypes


def mxq(x, axis, fmt="e4m3"):
    dtype, down = {"e4m3": (ml_dtypes.float8_e4m3fn, 7), "e5m2": (ml_dtypes.float8_e5m2, 14)}[fmt]
    v = np.moveaxis(np.asarray(x, np.float32).astype(ml_dtypes.bfloat16).astype(np.float64), axis, -1)
    blocks = v.reshape(v.shape[:-1] + (-1, 32))
    amax = np.abs(blocks).max(-1, keepdims=True)
    byte = np.maximum(np.where(amax > 0, np.frexp(amax)[1] - 1 + 127, 0) - down, 1)
    scale = np.exp2(byte - 127.0)
    codes = (blocks / scale).astype(np.float32).astype(dtype).astype(np.float64)
    return np.moveaxis((codes * scale).reshape(v.shape), -1, axis)


WIDE = False


def mx_kscale(k):
    if not WIDE:
        return np.ones(k)
    levels = np.array([10, -10, 5, -5, 0])
    if k % 512:
        return np.exp2(np.random.permutation(np.resize(levels, k // 32))).repeat(32)
    a = np.empty((k // 512, 16))
    for p in range(k // 512):
        a[p, :8] = np.random.permutation(np.resize(levels, 8))
        for g in range(8):
            far = levels[np.abs(levels - a[p, g]) >= 10]
            a[p, g + 8] = far[np.random.randint(len(far))]
    return np.exp2(a.ravel()).repeat(32)


def f64(x):
    return np.asarray(x).astype(np.float64)


def striped(idx):
    return np.tile(idx.reshape(-1, 16).T, (8, 1)).astype(np.uint16)


def unstriped(offs):
    return offs[:16].T.reshape(-1).astype(np.int64)


def pack_weight(w):
    k, n = w.shape
    w = f64(np.asarray(w, np.float32).astype(ml_dtypes.bfloat16)).reshape(k // 32, 32, n)
    amax = np.abs(w).max(1)
    byte = np.clip(np.where(amax > 0, np.frexp(amax)[1] - 1 + 127 - 7, 1), 1, 254)
    scaled = (w * np.exp2(127.0 - byte)[:, None, :]).reshape(k, n).astype(np.float32)
    words = np.ascontiguousarray(scaled.reshape(k // 512, 128, 4, n).transpose(0, 1, 3, 2)).astype(ml_dtypes.float8_e4m3fn).view(np.uint8)
    return words, np.ascontiguousarray(byte.astype(np.uint8).reshape(k // 512, 16, n))


def unpack_weight(words, scales):
    g, p, n, _ = words.shape
    vals = np.ascontiguousarray(words).view(ml_dtypes.float8_e4m3fn).astype(np.float64) * np.repeat(np.exp2(scales.astype(np.float64) - 127.0), 8, axis=1)[..., None]
    return vals.transpose(0, 1, 3, 2).reshape(g * 512, n)


def relu(v):
    return np.maximum(v, 0.0)


K, T, D, S, V, N = 512, 1024, 2, 1024, 512, 256


def setup_inputs():
    n = np.random.standard_normal
    s = mx_kscale(K)[:, None]
    words, scales = pack_weight(n((K, N)) / np.sqrt(K) / s)
    return {
        "xT": (n((K, T)) * s / np.sqrt(D)).astype(ml_dtypes.bfloat16).astype(np.float32),
        "w_words": words,
        "w_scales": scales,
        "b": (0.3 * n((N, 1))).astype(np.float32),
        "offs": striped(np.concatenate([np.random.permutation(T)[:V] for _ in range(D)])),
    }


def reference(xT, w_words, w_scales, b, offs):
    w = unpack_weight(w_words, w_scales)
    idx = unstriped(offs)
    x = sum(f64(xT)[:, idx[d * V:(d + 1) * V]] for d in range(D))
    return relu((w.T @ mxq(x, 0, "e4m3")) + f64(b))

@@ -1,0 +1,114 @@
+from contextlib import ExitStack
+
+import concourse.mybir as mybir
+
+K, T, D, V, N = 512, 1024, 2, 512, 256
+FLOPS = 2 * K * V * N
+
+F32 = mybir.dt.float32
+BF16 = mybir.dt.bfloat16
+U32 = mybir.dt.uint32
+I32 = mybir.dt.int32
+U16 = mybir.dt.uint16
+U8 = mybir.dt.uint8
+FP8X4 = mybir.dt.float8_e4m3fn_x4
+ADD = mybir.AluOpType.add
+MAX = mybir.AluOpType.max
+RELU = mybir.ActivationFunctionType.Relu
+COPY = mybir.ActivationFunctionType.Copy
+
+P = 128
+STRIPE = 16
+
+ID_CHUNKS = [(0, 256), (256, 384), (384, 512)]
+FIRST_LOADS = [(0, 512), (512, 1024)]
+PAIR_LOADS = [(0, 512), (512, 1024)]
+LAST_LOADS = [(0, 512), (512, 1024)]
+
+
+def tile_picked_hash_lin_relu_sub_l_kernel(tc, xT, w_words, w_scales, b, offs, out):
+    nc = tc.nc
+    with ExitStack() as ctx:
+        keep = ctx.enter_context(tc.tile_pool(name="keep", bufs=1))
+        ring = ctx.enter_context(tc.tile_pool(name="ring", bufs=2))
+        psum = ctx.enter_context(tc.psum_pool(name="psum", bufs=1))
+
+        offsets = keep.tile([P, D * V // STRIPE], U16, name="offsets")
+        w_codes = keep.tile([P, N], U32, name="w_codes", align_bytes=64)
+        w_plane = keep.tile([P, N], U8, name="w_plane", align_bytes=64)
+        bias = keep.tile([P, N // P], F32, name="bias")
+        warm_in = keep.tile([P, 1], F32, name="warm_in")
+        warm_out = keep.tile([P, 1], F32, name="warm_out")
+        singles = [keep.tile([P, T], BF16, name=f"single{e}") for e in range(2)]
+        pairs = keep.tile([P, T, 2], BF16, name="pairs")
+        picked = [keep.tile([P, 2, V, 2], BF16, name=f"picked{d}") for d in range(D)]
+
+        nc.gpsimd.memset(warm_in[:], 0.0)
+        nc.gpsimd.memset(w_plane[:].bitcast(I32), 0)
+        nc.scalar.activation(warm_out[:], warm_in[:], RELU)
+
+        x_rows = xT.rearrange("(p j) c -> p j c", j=4)
+
+        def load(name, j0, j1, spans):
+            tiles = []
+            for c0, c1 in spans:
+                tile = keep.tile([P, j1 - j0, c1 - c0], F32, name=f"{name}{c0}")
+                nc.sync.dma_start(tile[:], x_rows[:, j0:j1, c0:c1])
+                tiles.append(tile)
+            return tiles
+
+        raw_first = load("raw_first", 2, 3, FIRST_LOADS)
+        nc.sync.dma_start(offsets[:], offs)
+        raw_pair = load("raw_pair", 0, 2, PAIR_LOADS)
+        raw_last = load("raw_last", 3, 4, LAST_LOADS)
+        nc.sync.dma_start(w_codes[:].bitcast(I32), w_words[0].rearrange("p n t -> p (n t)").bitcast(I32))
+        for q in range(4):
+            nc.sync.dma_start(w_plane[32 * q : 32 * q + 4, :].bitcast(I32), w_scales[0, 4 * q : 4 * q + 4, :].bitcast(I32))
+        with nc.allow_non_contiguous_dma(reason="one bias value for each partition and half"):
+            nc.sync.dma_start(bias[:], b.rearrange("(c p) o -> p (c o)", p=P))
+
+        def list_columns(d, v0, v1):
+            return offsets[:, (d * V + v0) // STRIPE : (d * V + v1) // STRIPE]
+
+        def gather_single(e, d, v0, v1):
+            nc.scalar.activation(picked[d][:, 1, v0:v1, e], singles[e][:].indirect(list_columns(d, v0, v1)), COPY)
+
+        def gather_pair(d, v0, v1):
+            window = pairs[:].rearrange("p c e -> p (c e)").bitcast(U32)
+            dst = picked[d][:, 0, v0:v1, :].rearrange("p v e -> p (v e)").bitcast(U32)
+            nc.vector.tensor_copy(dst, window.indirect(list_columns(d, v0, v1)))
+
+        for tile, (c0, c1) in zip(raw_first, FIRST_LOADS):
+            nc.vector.tensor_copy(singles[0][:, c0:c1], tile[:, 0, :])
+        for d in range(D):
+            gather_single(0, d, 0, V)
+        for tile, (c0, c1) in zip(raw_pair, PAIR_LOADS):
+            nc.vector.tensor_copy(pairs[:, c0:c1, :], tile[:].rearrange("p e c -> p c e"))
+        for d in range(D):
+            gather_pair(d, 0, V)
+        for tile, (c0, c1) in zip(raw_last, LAST_LOADS):
+            nc.scalar.copy(singles[1][:, c0:c1], tile[:, 0, :])
+        for v0, v1 in ID_CHUNKS:
+            for d in range(D):
+                gather_single(1, d, v0, v1)
+
+        out_rows = out.rearrange("(m p) v -> p m v", p=P)
+        last = len(ID_CHUNKS) - 1
+        for c, (v0, v1) in enumerate(ID_CHUNKS):
+            width = v1 - v0
+            sums = ring.tile([P, width, 2, 2], BF16, name="sums", align_bytes=64)
+            a0, a1 = [picked[d][:, :, v0:v1, :].rearrange("p h v e -> p v h e") for d in range(D)]
+            nc.vector.tensor_tensor(sums[:], a0, a1, ADD)
+            x_codes = keep.tile([P, width], U32, name=f"x_codes{c}", align_bytes=64)
+            x_plane = keep.tile([P, width], U8, name=f"x_plane{c}", align_bytes=64)
+            nc.vector.quantize_mx(x_codes[:].bitcast(FP8X4), x_plane[:], sums[:].rearrange("p v h e -> p (v h e)"))
+            res = keep.tile([P, N // P, width], F32, name=f"res{c}")
+            for m in range(N // P):
+                cols = slice(m * P, (m + 1) * P)
+                acc = psum.tile([P, width], F32, name=f"acc{c}_{m}")
+                nc.tensor.matmul_mx(acc[:], w_codes[:, cols].bitcast(FP8X4), w_plane[:, cols], x_codes[:].bitcast(FP8X4), x_plane[:], start=True, stop=True)
+                if c == last and m == 1:
+                    nc.vector.tensor_scalar(res[:, m, :], acc[:], bias[:, m : m + 1], 0.0, ADD, MAX)
+                else:
+                    nc.scalar.activation(res[:, m, :], acc[:], RELU, bias=bias[:, m : m + 1])
+            nc.sync.dma_start(out_rows[:, :, v0:v1], res[:])

@@ -20,10 +20,16 @@ COPY = mybir.ActivationFunctionType.Copy
 P = 128
 STRIPE = 16
 
-ID_CHUNKS = [(0, 256), (256, 384), (384, 512)]
-FIRST_LOADS = [(0, 512), (512, 1024)]
-PAIR_LOADS = [(0, 512), (512, 1024)]
+ID_CHUNKS = [(0, 128), (128, 256), (256, 384), (384, 512)]
+VECTOR_PIECES = []
+SCALAR_FIRST = [(0, 0, 512), (1, 0, 512)]
+SCALAR_LAST = [(d, v0, v1) for v0, v1 in ID_CHUNKS for d in range(D)]
+FIRST_LOADS = [(0, 640), (640, 1024)]
+PAIR_LOADS = [(0, 640), (640, 1024)]
 LAST_LOADS = [(0, 512), (512, 1024)]
+GPSIMD_CASTS = [(0, 512), (832, 1024)]
+SCALAR_CASTS = [(512, 832)]
+MULT = mybir.AluOpType.mult
 
 
 def tile_picked_hash_lin_relu_sub_l_kernel(tc, xT, w_words, w_scales, b, offs, out):
@@ -39,6 +45,8 @@ def tile_picked_hash_lin_relu_sub_l_kernel(tc, xT, w_words, w_scales, b, offs, o
         bias = keep.tile([P, N // P], F32, name="bias")
         warm_in = keep.tile([P, 1], F32, name="warm_in")
         warm_out = keep.tile([P, 1], F32, name="warm_out")
+        raw_pair = keep.tile([P, 2, T], F32, name="raw_pair")
+        raw_single = [keep.tile([P, T], F32, name=f"raw_single{e}") for e in range(2)]
         singles = [keep.tile([P, T], BF16, name=f"single{e}") for e in range(2)]
         pairs = keep.tile([P, T, 2], BF16, name="pairs")
         picked = [keep.tile([P, 2, V, 2], BF16, name=f"picked{d}") for d in range(D)]
@@ -48,19 +56,13 @@ def tile_picked_hash_lin_relu_sub_l_kernel(tc, xT, w_words, w_scales, b, offs, o
         nc.scalar.activation(warm_out[:], warm_in[:], RELU)
 
         x_rows = xT.rearrange("(p j) c -> p j c", j=4)
-
-        def load(name, j0, j1, spans):
-            tiles = []
-            for c0, c1 in spans:
-                tile = keep.tile([P, j1 - j0, c1 - c0], F32, name=f"{name}{c0}")
-                nc.sync.dma_start(tile[:], x_rows[:, j0:j1, c0:c1])
-                tiles.append(tile)
-            return tiles
-
-        raw_first = load("raw_first", 2, 3, FIRST_LOADS)
+        for c0, c1 in FIRST_LOADS:
+            nc.sync.dma_start(raw_single[0][:, c0:c1], x_rows[:, 2, c0:c1])
         nc.sync.dma_start(offsets[:], offs)
-        raw_pair = load("raw_pair", 0, 2, PAIR_LOADS)
-        raw_last = load("raw_last", 3, 4, LAST_LOADS)
+        for c0, c1 in PAIR_LOADS:
+            nc.sync.dma_start(raw_pair[:, :, c0:c1], x_rows[:, 0:2, c0:c1])
+        for c0, c1 in LAST_LOADS:
+            nc.sync.dma_start(raw_single[1][:, c0:c1], x_rows[:, 3, c0:c1])
         nc.sync.dma_start(w_codes[:].bitcast(I32), w_words[0].rearrange("p n t -> p (n t)").bitcast(I32))
         for q in range(4):
             nc.sync.dma_start(w_plane[32 * q : 32 * q + 4, :].bitcast(I32), w_scales[0, 4 * q : 4 * q + 4, :].bitcast(I32))
@@ -70,27 +72,35 @@ def tile_picked_hash_lin_relu_sub_l_kernel(tc, xT, w_words, w_scales, b, offs, o
         def list_columns(d, v0, v1):
             return offsets[:, (d * V + v0) // STRIPE : (d * V + v1) // STRIPE]
 
-        def gather_single(e, d, v0, v1):
+        def scalar_gather(e, d, v0, v1):
             nc.scalar.activation(picked[d][:, 1, v0:v1, e], singles[e][:].indirect(list_columns(d, v0, v1)), COPY)
+
+        def vector_gather(e, d, v0, v1):
+            nc.vector.tensor_copy(picked[d][:, 1, v0:v1, e], raw_single[e][:].indirect(list_columns(d, v0, v1)))
 
         def gather_pair(d, v0, v1):
             window = pairs[:].rearrange("p c e -> p (c e)").bitcast(U32)
             dst = picked[d][:, 0, v0:v1, :].rearrange("p v e -> p (v e)").bitcast(U32)
             nc.vector.tensor_copy(dst, window.indirect(list_columns(d, v0, v1)))
 
-        for tile, (c0, c1) in zip(raw_first, FIRST_LOADS):
-            nc.vector.tensor_copy(singles[0][:, c0:c1], tile[:, 0, :])
-        for d in range(D):
-            gather_single(0, d, 0, V)
-        for tile, (c0, c1) in zip(raw_pair, PAIR_LOADS):
-            nc.vector.tensor_copy(pairs[:, c0:c1, :], tile[:].rearrange("p e c -> p c e"))
+        for c0, c1 in FIRST_LOADS:
+            nc.vector.tensor_copy(singles[0][:, c0:c1], raw_single[0][:, c0:c1])
+        for piece in SCALAR_FIRST:
+            scalar_gather(0, *piece)
+        for piece in VECTOR_PIECES:
+            vector_gather(0, *piece)
+        for c0, c1 in PAIR_LOADS:
+            nc.vector.tensor_copy(pairs[:, c0:c1, :], raw_pair[:, :, c0:c1].rearrange("p e c -> p c e"))
         for d in range(D):
             gather_pair(d, 0, V)
-        for tile, (c0, c1) in zip(raw_last, LAST_LOADS):
-            nc.scalar.copy(singles[1][:, c0:c1], tile[:, 0, :])
-        for v0, v1 in ID_CHUNKS:
-            for d in range(D):
-                gather_single(1, d, v0, v1)
+        for c0, c1 in GPSIMD_CASTS:
+            nc.gpsimd.tensor_scalar(singles[1][:, c0:c1], raw_single[1][:, c0:c1], 1.0, 0.0, MULT, ADD)
+        for c0, c1 in SCALAR_CASTS:
+            nc.scalar.copy(singles[1][:, c0:c1], raw_single[1][:, c0:c1])
+        for piece in SCALAR_LAST:
+            scalar_gather(1, *piece)
+        for piece in VECTOR_PIECES:
+            vector_gather(1, *piece)
 
         out_rows = out.rearrange("(m p) v -> p m v", p=P)
         last = len(ID_CHUNKS) - 1

@@ -14,29 +14,25 @@ U8 = mybir.dt.uint8
 FP8X4 = mybir.dt.float8_e4m3fn_x4
 ADD = mybir.AluOpType.add
 MAX = mybir.AluOpType.max
+MULT = mybir.AluOpType.mult
 RELU = mybir.ActivationFunctionType.Relu
 COPY = mybir.ActivationFunctionType.Copy
 
 P = 128
 STRIPE = 16
 
+ROWS = 4
 ID_CHUNKS = [(0, 128), (128, 256), (256, 384), (384, 512)]
-VECTOR_PIECES = []
-SCALAR_FIRST = [(0, 0, 512), (1, 0, 512)]
-SCALAR_LAST = [(d, v0, v1) for v0, v1 in ID_CHUNKS for d in range(D)]
-FIRST_LOADS = [(0, 640), (640, 1024)]
-PAIR_LOADS = [(0, 640), (640, 1024)]
-LAST_LOADS = [(0, 512), (512, 1024)]
-GPSIMD_CASTS = [(0, 512), (832, 1024)]
-SCALAR_CASTS = [(512, 832)]
-MULT = mybir.AluOpType.mult
+ROW_LOADS = [[(0, 1024)], [(0, 512), (512, 1024)], [(0, 1024)], [(0, 1024)]]
+SCALAR_LAST = [(0, 128), (128, 256), (256, 384), (384, 512)]
+FIRST_CAST_SPLIT = 576
+VECTOR_EPILOGUES = [(2, 1), (3, 1)]
 
 
 def tile_picked_hash_lin_relu_sub_l_kernel(tc, xT, w_words, w_scales, b, offs, out):
     nc = tc.nc
     with ExitStack() as ctx:
         keep = ctx.enter_context(tc.tile_pool(name="keep", bufs=1))
-        ring = ctx.enter_context(tc.tile_pool(name="ring", bufs=2))
         psum = ctx.enter_context(tc.psum_pool(name="psum", bufs=1))
 
         offsets = keep.tile([P, D * V // STRIPE], U16, name="offsets")
@@ -45,24 +41,20 @@ def tile_picked_hash_lin_relu_sub_l_kernel(tc, xT, w_words, w_scales, b, offs, o
         bias = keep.tile([P, N // P], F32, name="bias")
         warm_in = keep.tile([P, 1], F32, name="warm_in")
         warm_out = keep.tile([P, 1], F32, name="warm_out")
-        raw_pair = keep.tile([P, 2, T], F32, name="raw_pair")
-        raw_single = [keep.tile([P, T], F32, name=f"raw_single{e}") for e in range(2)]
-        singles = [keep.tile([P, T], BF16, name=f"single{e}") for e in range(2)]
-        pairs = keep.tile([P, T, 2], BF16, name="pairs")
+        raw = [keep.tile([P, T], F32, name=f"raw{t}") for t in range(ROWS)]
+        cast = [keep.tile([P, T], BF16, name=f"cast{t}") for t in range(ROWS)]
         picked = [keep.tile([P, 2, V, 2], BF16, name=f"picked{d}") for d in range(D)]
 
         nc.gpsimd.memset(warm_in[:], 0.0)
         nc.gpsimd.memset(w_plane[:].bitcast(I32), 0)
         nc.scalar.activation(warm_out[:], warm_in[:], RELU)
 
-        x_rows = xT.rearrange("(p j) c -> p j c", j=4)
-        for c0, c1 in FIRST_LOADS:
-            nc.sync.dma_start(raw_single[0][:, c0:c1], x_rows[:, 2, c0:c1])
-        nc.sync.dma_start(offsets[:], offs)
-        for c0, c1 in PAIR_LOADS:
-            nc.sync.dma_start(raw_pair[:, :, c0:c1], x_rows[:, 0:2, c0:c1])
-        for c0, c1 in LAST_LOADS:
-            nc.sync.dma_start(raw_single[1][:, c0:c1], x_rows[:, 3, c0:c1])
+        x_rows = xT.rearrange("(p j) c -> p j c", j=ROWS)
+        for t in range(ROWS):
+            for c0, c1 in ROW_LOADS[t]:
+                nc.sync.dma_start(raw[t][:, c0:c1], x_rows[:, t, c0:c1])
+            if t == 0:
+                nc.sync.dma_start(offsets[:], offs)
         nc.sync.dma_start(w_codes[:].bitcast(I32), w_words[0].rearrange("p n t -> p (n t)").bitcast(I32))
         for q in range(4):
             nc.sync.dma_start(w_plane[32 * q : 32 * q + 4, :].bitcast(I32), w_scales[0, 4 * q : 4 * q + 4, :].bitcast(I32))
@@ -72,41 +64,23 @@ def tile_picked_hash_lin_relu_sub_l_kernel(tc, xT, w_words, w_scales, b, offs, o
         def list_columns(d, v0, v1):
             return offsets[:, (d * V + v0) // STRIPE : (d * V + v1) // STRIPE]
 
-        def scalar_gather(e, d, v0, v1):
-            nc.scalar.activation(picked[d][:, 1, v0:v1, e], singles[e][:].indirect(list_columns(d, v0, v1)), COPY)
+        def gpsimd_cast(t, c0, c1):
+            nc.gpsimd.tensor_scalar(cast[t][:, c0:c1], raw[t][:, c0:c1], 1.0, 0.0, MULT, ADD)
 
-        def vector_gather(e, d, v0, v1):
-            nc.vector.tensor_copy(picked[d][:, 1, v0:v1, e], raw_single[e][:].indirect(list_columns(d, v0, v1)))
-
-        def gather_pair(d, v0, v1):
-            window = pairs[:].rearrange("p c e -> p (c e)").bitcast(U32)
-            dst = picked[d][:, 0, v0:v1, :].rearrange("p v e -> p (v e)").bitcast(U32)
-            nc.vector.tensor_copy(dst, window.indirect(list_columns(d, v0, v1)))
-
-        for c0, c1 in FIRST_LOADS:
-            nc.vector.tensor_copy(singles[0][:, c0:c1], raw_single[0][:, c0:c1])
-        for piece in SCALAR_FIRST:
-            scalar_gather(0, *piece)
-        for piece in VECTOR_PIECES:
-            vector_gather(0, *piece)
-        for c0, c1 in PAIR_LOADS:
-            nc.vector.tensor_copy(pairs[:, c0:c1, :], raw_pair[:, :, c0:c1].rearrange("p e c -> p c e"))
-        for d in range(D):
-            gather_pair(d, 0, V)
-        for c0, c1 in GPSIMD_CASTS:
-            nc.gpsimd.tensor_scalar(singles[1][:, c0:c1], raw_single[1][:, c0:c1], 1.0, 0.0, MULT, ADD)
-        for c0, c1 in SCALAR_CASTS:
-            nc.scalar.copy(singles[1][:, c0:c1], raw_single[1][:, c0:c1])
-        for piece in SCALAR_LAST:
-            scalar_gather(1, *piece)
-        for piece in VECTOR_PIECES:
-            vector_gather(1, *piece)
+        nc.scalar.copy(cast[0][:, :FIRST_CAST_SPLIT], raw[0][:, :FIRST_CAST_SPLIT])
+        gpsimd_cast(0, FIRST_CAST_SPLIT, T)
+        for t in range(ROWS):
+            if t > 0:
+                for c0, c1 in ROW_LOADS[t]:
+                    gpsimd_cast(t, c0, c1)
+            nc.vector.tensor_copy(picked[0][:, t // 2, :, t % 2], raw[t][:].indirect(list_columns(0, 0, V)))
+            for v0, v1 in SCALAR_LAST if t == ROWS - 1 else [(0, V)]:
+                nc.scalar.activation(picked[1][:, t // 2, v0:v1, t % 2], cast[t][:].indirect(list_columns(1, v0, v1)), COPY)
 
         out_rows = out.rearrange("(m p) v -> p m v", p=P)
-        last = len(ID_CHUNKS) - 1
         for c, (v0, v1) in enumerate(ID_CHUNKS):
             width = v1 - v0
-            sums = ring.tile([P, width, 2, 2], BF16, name="sums", align_bytes=64)
+            sums = keep.tile([P, width, 2, 2], BF16, name=f"sums{c}", align_bytes=64)
             a0, a1 = [picked[d][:, :, v0:v1, :].rearrange("p h v e -> p v h e") for d in range(D)]
             nc.vector.tensor_tensor(sums[:], a0, a1, ADD)
             x_codes = keep.tile([P, width], U32, name=f"x_codes{c}", align_bytes=64)
@@ -117,7 +91,7 @@ def tile_picked_hash_lin_relu_sub_l_kernel(tc, xT, w_words, w_scales, b, offs, o
                 cols = slice(m * P, (m + 1) * P)
                 acc = psum.tile([P, width], F32, name=f"acc{c}_{m}")
                 nc.tensor.matmul_mx(acc[:], w_codes[:, cols].bitcast(FP8X4), w_plane[:, cols], x_codes[:].bitcast(FP8X4), x_plane[:], start=True, stop=True)
-                if c == last and m == 1:
+                if (c, m) in VECTOR_EPILOGUES:
                     nc.vector.tensor_scalar(res[:, m, :], acc[:], bias[:, m : m + 1], 0.0, ADD, MAX)
                 else:
                     nc.scalar.activation(res[:, m, :], acc[:], RELU, bias=bias[:, m : m + 1])

@@ -24,7 +24,8 @@ STRIPE = 16
 ROWS = 4
 ID_CHUNKS = [(0, 128), (128, 256), (256, 384), (384, 512)]
 ROW_LOADS = [[(0, 1024)], [(0, 512), (512, 1024)], [(0, 1024)], [(0, 1024)]]
-SCALAR_LAST = [(0, 128), (128, 256), (256, 384), (384, 512)]
+VECTOR_PIECES = [[(0, 448)], [(0, 448)], [(0, 384), (512, 640)], [(0, 384), (512, 640)]]
+SCALAR_PIECES = [[(448, 1024)], [(448, 1024)], [(384, 512), (640, 1024)], [(640, 768), (768, 896), (384, 512), (896, 1024)]]
 FIRST_CAST_SPLIT = 576
 VECTOR_EPILOGUES = [(2, 1), (3, 1)]
 
@@ -42,8 +43,9 @@ def tile_picked_hash_lin_relu_sub_l_kernel(tc, xT, w_words, w_scales, b, offs, o
         warm_in = keep.tile([P, 1], F32, name="warm_in")
         warm_out = keep.tile([P, 1], F32, name="warm_out")
         raw = [keep.tile([P, T], F32, name=f"raw{t}") for t in range(ROWS)]
-        cast = [keep.tile([P, T], BF16, name=f"cast{t}") for t in range(ROWS)]
-        picked = [keep.tile([P, 2, V, 2], BF16, name=f"picked{d}") for d in range(D)]
+        cast = [keep.tile([P, T], BF16, name=f"cast{t}") for t in range(ROWS - 1)]
+        cast.append(keep.tile([P, T], BF16, name="cast_last", tag="late"))
+        picked = keep.tile([P, 2, D * V, 2], BF16, name="picked")
 
         nc.gpsimd.memset(warm_in[:], 0.0)
         nc.gpsimd.memset(w_plane[:].bitcast(I32), 0)
@@ -61,8 +63,8 @@ def tile_picked_hash_lin_relu_sub_l_kernel(tc, xT, w_words, w_scales, b, offs, o
         with nc.allow_non_contiguous_dma(reason="one bias value for each partition and half"):
             nc.sync.dma_start(bias[:], b.rearrange("(c p) o -> p (c o)", p=P))
 
-        def list_columns(d, v0, v1):
-            return offsets[:, (d * V + v0) // STRIPE : (d * V + v1) // STRIPE]
+        def list_columns(j0, j1):
+            return offsets[:, j0 // STRIPE : j1 // STRIPE]
 
         def gpsimd_cast(t, c0, c1):
             nc.gpsimd.tensor_scalar(cast[t][:, c0:c1], raw[t][:, c0:c1], 1.0, 0.0, MULT, ADD)
@@ -73,20 +75,21 @@ def tile_picked_hash_lin_relu_sub_l_kernel(tc, xT, w_words, w_scales, b, offs, o
             if t > 0:
                 for c0, c1 in ROW_LOADS[t]:
                     gpsimd_cast(t, c0, c1)
-            nc.vector.tensor_copy(picked[0][:, t // 2, :, t % 2], raw[t][:].indirect(list_columns(0, 0, V)))
-            for v0, v1 in SCALAR_LAST if t == ROWS - 1 else [(0, V)]:
-                nc.scalar.activation(picked[1][:, t // 2, v0:v1, t % 2], cast[t][:].indirect(list_columns(1, v0, v1)), COPY)
+            for j0, j1 in VECTOR_PIECES[t]:
+                nc.vector.tensor_copy(picked[:, t // 2, j0:j1, t % 2], raw[t][:].indirect(list_columns(j0, j1)))
+            for j0, j1 in SCALAR_PIECES[t]:
+                nc.scalar.activation(picked[:, t // 2, j0:j1, t % 2], cast[t][:].indirect(list_columns(j0, j1)), COPY)
 
         out_rows = out.rearrange("(m p) v -> p m v", p=P)
         for c, (v0, v1) in enumerate(ID_CHUNKS):
             width = v1 - v0
             sums = keep.tile([P, width, 2, 2], BF16, name=f"sums{c}", align_bytes=64)
-            a0, a1 = [picked[d][:, :, v0:v1, :].rearrange("p h v e -> p v h e") for d in range(D)]
+            a0, a1 = [picked[:, :, d * V + v0 : d * V + v1, :].rearrange("p h v e -> p v h e") for d in range(D)]
             nc.vector.tensor_tensor(sums[:], a0, a1, ADD)
             x_codes = keep.tile([P, width], U32, name=f"x_codes{c}", align_bytes=64)
             x_plane = keep.tile([P, width], U8, name=f"x_plane{c}", align_bytes=64)
             nc.vector.quantize_mx(x_codes[:].bitcast(FP8X4), x_plane[:], sums[:].rearrange("p v h e -> p (v h e)"))
-            res = keep.tile([P, N // P, width], F32, name=f"res{c}")
+            res = keep.tile([P, N // P, width], F32, name=f"res{c}", tag="late" if c == 0 else f"res{c}")
             for m in range(N // P):
                 cols = slice(m * P, (m + 1) * P)
                 acc = psum.tile([P, width], F32, name=f"acc{c}_{m}")

@@ -19,15 +19,22 @@ RELU = mybir.ActivationFunctionType.Relu
 COPY = mybir.ActivationFunctionType.Copy
 
 P = 128
-STRIPE = 16
-
 ROWS = 4
-ID_CHUNKS = [(0, 128), (128, 256), (256, 384), (384, 512)]
-ROW_LOADS = [[(0, 1024)], [(0, 512), (512, 1024)], [(0, 1024)], [(0, 1024)]]
-VECTOR_PIECES = [[(0, 448)], [(0, 448)], [(0, 384), (512, 640)], [(0, 384), (512, 640)]]
-SCALAR_PIECES = [[(448, 1024)], [(448, 1024)], [(384, 512), (640, 1024)], [(640, 768), (768, 896), (384, 512), (896, 1024)]]
+STRIPE = 16
+ENTRIES = D * V
+CHUNK = 128
+CHUNKS = V // CHUNK
+
+ROW_LOADS = [[(0, T)], [(0, T // 2), (T // 2, T)], [(0, T)], [(0, T)]]
 FIRST_CAST_SPLIT = 576
-VECTOR_EPILOGUES = [(2, 1), (3, 1)]
+EARLY_SPLIT = 416
+EARLY_VECTOR, EARLY_SCALAR = [(0, EARLY_SPLIT)], [(EARLY_SPLIT, ENTRIES)]
+LATE_VECTOR = [(0, V - CHUNK), (V, V + CHUNK)]
+LATE_SCALAR = [(V - CHUNK, V), (V + CHUNK, ENTRIES)]
+LAST_SCALAR = [(V + CHUNK, V + 3 * CHUNK), (V - CHUNK, V), (V + 3 * CHUNK, ENTRIES)]
+VECTOR_PIECES = [EARLY_VECTOR, EARLY_VECTOR, LATE_VECTOR, LATE_VECTOR]
+SCALAR_PIECES = [EARLY_SCALAR, EARLY_SCALAR, LATE_SCALAR, LAST_SCALAR]
+VECTOR_EPILOGUES = [(CHUNKS - 2, 1), (CHUNKS - 1, 1)]
 
 
 def tile_picked_hash_lin_relu_sub_l_kernel(tc, xT, w_words, w_scales, b, offs, out):
@@ -36,7 +43,7 @@ def tile_picked_hash_lin_relu_sub_l_kernel(tc, xT, w_words, w_scales, b, offs, o
         keep = ctx.enter_context(tc.tile_pool(name="keep", bufs=1))
         psum = ctx.enter_context(tc.psum_pool(name="psum", bufs=1))
 
-        offsets = keep.tile([P, D * V // STRIPE], U16, name="offsets")
+        offsets = keep.tile([P, ENTRIES // STRIPE], U16, name="offsets")
         w_codes = keep.tile([P, N], U32, name="w_codes", align_bytes=64)
         w_plane = keep.tile([P, N], U8, name="w_plane", align_bytes=64)
         bias = keep.tile([P, N // P], F32, name="bias")
@@ -45,7 +52,7 @@ def tile_picked_hash_lin_relu_sub_l_kernel(tc, xT, w_words, w_scales, b, offs, o
         raw = [keep.tile([P, T], F32, name=f"raw{t}") for t in range(ROWS)]
         cast = [keep.tile([P, T], BF16, name=f"cast{t}") for t in range(ROWS - 1)]
         cast.append(keep.tile([P, T], BF16, name="cast_last", tag="late"))
-        picked = keep.tile([P, 2, D * V, 2], BF16, name="picked")
+        picked = keep.tile([P, 2, ENTRIES, 2], BF16, name="picked")
 
         nc.gpsimd.memset(warm_in[:], 0.0)
         nc.gpsimd.memset(w_plane[:].bitcast(I32), 0)
@@ -81,18 +88,22 @@ def tile_picked_hash_lin_relu_sub_l_kernel(tc, xT, w_words, w_scales, b, offs, o
                 nc.scalar.activation(picked[:, t // 2, j0:j1, t % 2], cast[t][:].indirect(list_columns(j0, j1)), COPY)
 
         out_rows = out.rearrange("(m p) v -> p m v", p=P)
-        for c, (v0, v1) in enumerate(ID_CHUNKS):
-            width = v1 - v0
-            sums = keep.tile([P, width, 2, 2], BF16, name=f"sums{c}", align_bytes=64)
-            a0, a1 = [picked[:, :, d * V + v0 : d * V + v1, :].rearrange("p h v e -> p v h e") for d in range(D)]
-            nc.vector.tensor_tensor(sums[:], a0, a1, ADD)
-            x_codes = keep.tile([P, width], U32, name=f"x_codes{c}", align_bytes=64)
-            x_plane = keep.tile([P, width], U8, name=f"x_plane{c}", align_bytes=64)
-            nc.vector.quantize_mx(x_codes[:].bitcast(FP8X4), x_plane[:], sums[:].rearrange("p v h e -> p (v h e)"))
-            res = keep.tile([P, N // P, width], F32, name=f"res{c}", tag="late" if c == 0 else f"res{c}")
+        for c in range(CHUNKS):
+            v0, v1 = c * CHUNK, (c + 1) * CHUNK
+            sums = keep.tile([P, CHUNK, 2, 2], BF16, name=f"sums{c}", align_bytes=64)
+            x_codes = keep.tile([P, CHUNK], U32, name=f"x_codes{c}", align_bytes=64)
+            x_plane = keep.tile([P, CHUNK], U8, name=f"x_plane{c}", align_bytes=64)
+            step = CHUNK // 2 if c == 0 else CHUNK
+            parts = [(s0, s0 + step) for s0 in range(0, CHUNK, step)]
+            for s0, s1 in parts:
+                a0, a1 = [picked[:, :, d * V + v0 + s0 : d * V + v0 + s1, :].rearrange("p h v e -> p v h e") for d in range(D)]
+                nc.vector.tensor_tensor(sums[:, s0:s1], a0, a1, ADD)
+            for s0, s1 in parts:
+                nc.vector.quantize_mx(x_codes[:, s0:s1].bitcast(FP8X4), x_plane[:, s0:s1], sums[:, s0:s1].rearrange("p v h e -> p (v h e)"))
+            res = keep.tile([P, N // P, CHUNK], F32, name=f"res{c}", tag="late" if c == 0 else f"res{c}")
             for m in range(N // P):
                 cols = slice(m * P, (m + 1) * P)
-                acc = psum.tile([P, width], F32, name=f"acc{c}_{m}")
+                acc = psum.tile([P, CHUNK], F32, name=f"acc{c}_{m}")
                 nc.tensor.matmul_mx(acc[:], w_codes[:, cols].bitcast(FP8X4), w_plane[:, cols], x_codes[:].bitcast(FP8X4), x_plane[:], start=True, stop=True)
                 if (c, m) in VECTOR_EPILOGUES:
                     nc.vector.tensor_scalar(res[:, m, :], acc[:], bias[:, m : m + 1], 0.0, ADD, MAX)

@@ -47,16 +47,12 @@ def tile_picked_hash_lin_relu_sub_l_kernel(tc, xT, w_words, w_scales, b, offs, o
         w_codes = keep.tile([P, N], U32, name="w_codes", align_bytes=64)
         w_plane = keep.tile([P, N], U8, name="w_plane", align_bytes=64)
         bias = keep.tile([P, N // P], F32, name="bias")
-        warm_in = keep.tile([P, 1], F32, name="warm_in")
-        warm_out = keep.tile([P, 1], F32, name="warm_out")
         raw = [keep.tile([P, T], F32, name=f"raw{t}") for t in range(ROWS)]
         cast = [keep.tile([P, T], BF16, name=f"cast{t}") for t in range(ROWS - 1)]
         cast.append(keep.tile([P, T], BF16, name="cast_last", tag="late"))
         picked = keep.tile([P, 2, ENTRIES, 2], BF16, name="picked")
 
-        nc.gpsimd.memset(warm_in[:], 0.0)
         nc.gpsimd.memset(w_plane[:].bitcast(I32), 0)
-        nc.scalar.activation(warm_out[:], warm_in[:], RELU)
 
         x_rows = xT.rearrange("(p j) c -> p j c", j=ROWS)
         for t in range(ROWS):

@@ -29,9 +29,9 @@ ROW_LOADS = [[(0, T)], [(0, T // 2), (T // 2, T)], [(0, T)], [(0, T)]]
 FIRST_CAST_SPLIT = 576
 EARLY_SPLIT = 416
 EARLY_VECTOR, EARLY_SCALAR = [(0, EARLY_SPLIT)], [(EARLY_SPLIT, ENTRIES)]
-LATE_VECTOR = [(0, V - CHUNK), (V, V + CHUNK)]
-LATE_SCALAR = [(V - CHUNK, V), (V + CHUNK, ENTRIES)]
-LAST_SCALAR = [(V + CHUNK, V + 3 * CHUNK), (V - CHUNK, V), (V + 3 * CHUNK, ENTRIES)]
+LATE_VECTOR = [(0, V // 2), (V, V + V // 2)]
+LATE_SCALAR = [(V // 2, V), (V + V // 2, ENTRIES)]
+LAST_SCALAR = [(V // 2, V), (V + 2 * CHUNK, V + 3 * CHUNK), (V + 3 * CHUNK, ENTRIES)]
 VECTOR_PIECES = [EARLY_VECTOR, EARLY_VECTOR, LATE_VECTOR, LATE_VECTOR]
 SCALAR_PIECES = [EARLY_SCALAR, EARLY_SCALAR, LATE_SCALAR, LAST_SCALAR]
 VECTOR_EPILOGUES = [(CHUNKS - 2, 1), (CHUNKS - 1, 1)]
@@ -89,14 +89,16 @@ def tile_picked_hash_lin_relu_sub_l_kernel(tc, xT, w_words, w_scales, b, offs, o
             sums = keep.tile([P, CHUNK, 2, 2], BF16, name=f"sums{c}", align_bytes=64)
             x_codes = keep.tile([P, CHUNK], U32, name=f"x_codes{c}", align_bytes=64)
             x_plane = keep.tile([P, CHUNK], U8, name=f"x_plane{c}", align_bytes=64)
-            step = CHUNK // 2 if c == 0 else CHUNK
+            step = CHUNK
             parts = [(s0, s0 + step) for s0 in range(0, CHUNK, step)]
             for s0, s1 in parts:
                 a0, a1 = [picked[:, :, d * V + v0 + s0 : d * V + v0 + s1, :].rearrange("p h v e -> p v h e") for d in range(D)]
                 nc.vector.tensor_tensor(sums[:, s0:s1], a0, a1, ADD)
             for s0, s1 in parts:
                 nc.vector.quantize_mx(x_codes[:, s0:s1].bitcast(FP8X4), x_plane[:, s0:s1], sums[:, s0:s1].rearrange("p v h e -> p (v h e)"))
-            res = keep.tile([P, N // P, CHUNK], F32, name=f"res{c}", tag="late" if c == 0 else f"res{c}")
+            if c == 0:
+                first_two = keep.tile([P, 2, N // P, CHUNK], F32, name="first_two", tag="late")
+            res = first_two[:, c] if c < 2 else keep.tile([P, N // P, CHUNK], F32, name=f"res{c}")[:]
             for m in range(N // P):
                 cols = slice(m * P, (m + 1) * P)
                 acc = psum.tile([P, CHUNK], F32, name=f"acc{c}_{m}")
@@ -105,4 +107,4 @@ def tile_picked_hash_lin_relu_sub_l_kernel(tc, xT, w_words, w_scales, b, offs, o
                     nc.vector.tensor_scalar(res[:, m, :], acc[:], bias[:, m : m + 1], 0.0, ADD, MAX)
                 else:
                     nc.scalar.activation(res[:, m, :], acc[:], RELU, bias=bias[:, m : m + 1])
-            nc.sync.dma_start(out_rows[:, :, v0:v1], res[:])
+            nc.sync.dma_start(out_rows[:, :, v0:v1], res)

@@ -27,12 +27,13 @@ CHUNKS = V // CHUNK
 
 ROW_LOADS = [[(0, T)], [(0, T // 2), (T // 2, T)], [(0, T)], [(0, T)]]
 FIRST_CAST_SPLIT = 576
-EARLY_SPLIT = 416
+EARLY_SPLIT = 480
 EARLY_VECTOR, EARLY_SCALAR = [(0, EARLY_SPLIT)], [(EARLY_SPLIT, ENTRIES)]
 LATE_VECTOR = [(0, V // 2), (V, V + V // 2)]
 LATE_SCALAR = [(V // 2, V), (V + V // 2, ENTRIES)]
 LAST_SCALAR = [(V // 2, V), (V + 2 * CHUNK, V + 3 * CHUNK), (V + 3 * CHUNK, ENTRIES)]
-VECTOR_PIECES = [EARLY_VECTOR, EARLY_VECTOR, LATE_VECTOR, LATE_VECTOR]
+LAST_VECTOR = [(0, V // 2), (V, V + CHUNK), (V + CHUNK, V + 2 * CHUNK)]
+VECTOR_PIECES = [EARLY_VECTOR, EARLY_VECTOR, LATE_VECTOR, LAST_VECTOR]
 SCALAR_PIECES = [EARLY_SCALAR, EARLY_SCALAR, LATE_SCALAR, LAST_SCALAR]
 VECTOR_EPILOGUES = [(CHUNKS - 2, 1), (CHUNKS - 1, 1)]
 

@@ -29,10 +29,11 @@ ROW_LOADS = [[(0, T)], [(0, T // 2), (T // 2, T)], [(0, T)], [(0, T)]]
 FIRST_CAST_SPLIT = 576
 EARLY_SPLIT = 480
 EARLY_VECTOR, EARLY_SCALAR = [(0, EARLY_SPLIT)], [(EARLY_SPLIT, ENTRIES)]
-LATE_VECTOR = [(0, V // 2), (V, V + V // 2)]
-LATE_SCALAR = [(V // 2, V), (V + V // 2, ENTRIES)]
-LAST_SCALAR = [(V // 2, V), (V + 2 * CHUNK, V + 3 * CHUNK), (V + 3 * CHUNK, ENTRIES)]
-LAST_VECTOR = [(0, V // 2), (V, V + CHUNK), (V + CHUNK, V + 2 * CHUNK)]
+LATE_SPLIT = V // 2 + 32
+LATE_VECTOR = [(0, LATE_SPLIT), (V, V + V // 2)]
+LATE_SCALAR = [(LATE_SPLIT, V), (V + V // 2, ENTRIES)]
+LAST_SCALAR = [(LATE_SPLIT, V), (V + 2 * CHUNK, V + 3 * CHUNK), (V + 3 * CHUNK, ENTRIES)]
+LAST_VECTOR = [(0, LATE_SPLIT), (V, V + CHUNK), (V + CHUNK, V + 2 * CHUNK)]
 VECTOR_PIECES = [EARLY_VECTOR, EARLY_VECTOR, LATE_VECTOR, LAST_VECTOR]
 SCALAR_PIECES = [EARLY_SCALAR, EARLY_SCALAR, LATE_SCALAR, LAST_SCALAR]
 VECTOR_EPILOGUES = [(CHUNKS - 2, 1), (CHUNKS - 1, 1)]
@@ -98,8 +99,8 @@ def tile_picked_hash_lin_relu_sub_l_kernel(tc, xT, w_words, w_scales, b, offs, o
             for s0, s1 in parts:
                 nc.vector.quantize_mx(x_codes[:, s0:s1].bitcast(FP8X4), x_plane[:, s0:s1], sums[:, s0:s1].rearrange("p v h e -> p (v h e)"))
             if c == 0:
-                first_two = keep.tile([P, 2, N // P, CHUNK], F32, name="first_two", tag="late")
-            res = first_two[:, c] if c < 2 else keep.tile([P, N // P, CHUNK], F32, name=f"res{c}")[:]
+                first_two = keep.tile([P, N // P, 2 * CHUNK], F32, name="first_two", tag="late")
+            res = first_two[:, :, v0:v1] if c < 2 else keep.tile([P, N // P, CHUNK], F32, name=f"res{c}")[:]
             for m in range(N // P):
                 cols = slice(m * P, (m + 1) * P)
                 acc = psum.tile([P, CHUNK], F32, name=f"acc{c}_{m}")
@@ -108,4 +109,9 @@ def tile_picked_hash_lin_relu_sub_l_kernel(tc, xT, w_words, w_scales, b, offs, o
                     nc.vector.tensor_scalar(res[:, m, :], acc[:], bias[:, m : m + 1], 0.0, ADD, MAX)
                 else:
                     nc.scalar.activation(res[:, m, :], acc[:], RELU, bias=bias[:, m : m + 1])
-            nc.sync.dma_start(out_rows[:, :, v0:v1], res)
+                if c == CHUNKS - 1:
+                    nc.sync.dma_start(out_rows[:, m, v0:v1], res[:, m, :])
+            if c == 1:
+                nc.sync.dma_start(out_rows[:, :, :v1], first_two[:])
+            elif c == 2:
+                nc.sync.dma_start(out_rows[:, :, v0:v1], res)

@@ -27,6 +27,7 @@ CHUNKS = V // CHUNK
 
 ROW_LOADS = [[(0, T)], [(0, T // 2), (T // 2, T)], [(0, T)], [(0, T)]]
 FIRST_CAST_SPLIT = 576
+LAST_CAST_SPLIT = 128
 EARLY_SPLIT = 480
 EARLY_VECTOR, EARLY_SCALAR = [(0, EARLY_SPLIT)], [(EARLY_SPLIT, ENTRIES)]
 LATE_SPLIT = V // 2 + 32
@@ -49,9 +50,8 @@ def tile_picked_hash_lin_relu_sub_l_kernel(tc, xT, w_words, w_scales, b, offs, o
         w_codes = keep.tile([P, N], U32, name="w_codes", align_bytes=64)
         w_plane = keep.tile([P, N], U8, name="w_plane", align_bytes=64)
         bias = keep.tile([P, N // P], F32, name="bias")
-        raw = [keep.tile([P, T], F32, name=f"raw{t}") for t in range(ROWS)]
+        raw = [keep.tile([P, T], F32, name=f"raw{t}", tag="late" if t == 1 else f"raw{t}") for t in range(ROWS)]
         cast = [keep.tile([P, T], BF16, name=f"cast{t}") for t in range(ROWS - 1)]
-        cast.append(keep.tile([P, T], BF16, name="cast_last", tag="late"))
         picked = keep.tile([P, 2, ENTRIES, 2], BF16, name="picked")
 
         nc.gpsimd.memset(w_plane[:].bitcast(I32), 0)
@@ -64,7 +64,8 @@ def tile_picked_hash_lin_relu_sub_l_kernel(tc, xT, w_words, w_scales, b, offs, o
                 nc.sync.dma_start(offsets[:], offs)
         nc.sync.dma_start(w_codes[:].bitcast(I32), w_words[0].rearrange("p n t -> p (n t)").bitcast(I32))
         for q in range(4):
-            nc.sync.dma_start(w_plane[32 * q : 32 * q + 4, :].bitcast(I32), w_scales[0, 4 * q : 4 * q + 4, :].bitcast(I32))
+            queue = nc.gpsimd if q == 0 else nc.sync
+            queue.dma_start(w_plane[32 * q : 32 * q + 4, :].bitcast(I32), w_scales[0, 4 * q : 4 * q + 4, :].bitcast(I32))
         with nc.allow_non_contiguous_dma(reason="one bias value for each partition and half"):
             nc.sync.dma_start(bias[:], b.rearrange("(c p) o -> p (c o)", p=P))
 
@@ -77,7 +78,12 @@ def tile_picked_hash_lin_relu_sub_l_kernel(tc, xT, w_words, w_scales, b, offs, o
         nc.scalar.copy(cast[0][:, :FIRST_CAST_SPLIT], raw[0][:, :FIRST_CAST_SPLIT])
         gpsimd_cast(0, FIRST_CAST_SPLIT, T)
         for t in range(ROWS):
-            if t > 0:
+            if t == 2:
+                cast.append(keep.tile([P, T], BF16, name="cast_last", tag="late"))
+                nc.scalar.copy(cast[3][:, :LAST_CAST_SPLIT], raw[3][:, :LAST_CAST_SPLIT])
+            if t == 3:
+                gpsimd_cast(t, LAST_CAST_SPLIT, T)
+            elif t > 0:
                 for c0, c1 in ROW_LOADS[t]:
                     gpsimd_cast(t, c0, c1)
             for j0, j1 in VECTOR_PIECES[t]:
@@ -109,9 +115,7 @@ def tile_picked_hash_lin_relu_sub_l_kernel(tc, xT, w_words, w_scales, b, offs, o
                     nc.vector.tensor_scalar(res[:, m, :], acc[:], bias[:, m : m + 1], 0.0, ADD, MAX)
                 else:
                     nc.scalar.activation(res[:, m, :], acc[:], RELU, bias=bias[:, m : m + 1])
-                if c == CHUNKS - 1:
+                if c >= 2:
                     nc.sync.dma_start(out_rows[:, m, v0:v1], res[:, m, :])
             if c == 1:
                 nc.sync.dma_start(out_rows[:, :, :v1], first_two[:])
-            elif c == 2:
-                nc.sync.dma_start(out_rows[:, :, v0:v1], res)

@@ -28,7 +28,7 @@ CHUNKS = V // CHUNK
 ROW_LOADS = [[(0, T)], [(0, T // 2), (T // 2, T)], [(0, T)], [(0, T)]]
 FIRST_CAST_SPLIT = 576
 LAST_CAST_SPLIT = 128
-EARLY_SPLIT = 480
+EARLY_SPLIT = 448
 EARLY_VECTOR, EARLY_SCALAR = [(0, EARLY_SPLIT)], [(EARLY_SPLIT, ENTRIES)]
 LATE_SPLIT = V // 2 + 32
 LATE_VECTOR = [(0, LATE_SPLIT), (V, V + V // 2)]
@@ -64,8 +64,7 @@ def tile_picked_hash_lin_relu_sub_l_kernel(tc, xT, w_words, w_scales, b, offs, o
                 nc.sync.dma_start(offsets[:], offs)
         nc.sync.dma_start(w_codes[:].bitcast(I32), w_words[0].rearrange("p n t -> p (n t)").bitcast(I32))
         for q in range(4):
-            queue = nc.gpsimd if q == 0 else nc.sync
-            queue.dma_start(w_plane[32 * q : 32 * q + 4, :].bitcast(I32), w_scales[0, 4 * q : 4 * q + 4, :].bitcast(I32))
+            nc.sync.dma_start(w_plane[32 * q : 32 * q + 4, :].bitcast(I32), w_scales[0, 4 * q : 4 * q + 4, :].bitcast(I32))
         with nc.allow_non_contiguous_dma(reason="one bias value for each partition and half"):
             nc.sync.dma_start(bias[:], b.rearrange("(c p) o -> p (c o)", p=P))
 
@@ -97,7 +96,7 @@ def tile_picked_hash_lin_relu_sub_l_kernel(tc, xT, w_words, w_scales, b, offs, o
             sums = keep.tile([P, CHUNK, 2, 2], BF16, name=f"sums{c}", align_bytes=64)
             x_codes = keep.tile([P, CHUNK], U32, name=f"x_codes{c}", align_bytes=64)
             x_plane = keep.tile([P, CHUNK], U8, name=f"x_plane{c}", align_bytes=64)
-            step = CHUNK
+            step = CHUNK // 2 if c == CHUNKS - 1 else CHUNK
             parts = [(s0, s0 + step) for s0 in range(0, CHUNK, step)]
             for s0, s1 in parts:
                 a0, a1 = [picked[:, :, d * V + v0 + s0 : d * V + v0 + s1, :].rearrange("p h v e -> p v h e") for d in range(D)]
@@ -115,7 +114,9 @@ def tile_picked_hash_lin_relu_sub_l_kernel(tc, xT, w_words, w_scales, b, offs, o
                     nc.vector.tensor_scalar(res[:, m, :], acc[:], bias[:, m : m + 1], 0.0, ADD, MAX)
                 else:
                     nc.scalar.activation(res[:, m, :], acc[:], RELU, bias=bias[:, m : m + 1])
-                if c >= 2:
+                if c == CHUNKS - 1:
                     nc.sync.dma_start(out_rows[:, m, v0:v1], res[:, m, :])
             if c == 1:
                 nc.sync.dma_start(out_rows[:, :, :v1], first_two[:])
+            elif c == 2:
+                nc.sync.dma_start(out_rows[:, :, v0:v1], res)

@@ -25,8 +25,8 @@ ENTRIES = D * V
 CHUNK = 128
 CHUNKS = V // CHUNK
 
-ROW_LOADS = [[(0, T)], [(0, T // 2), (T // 2, T)], [(0, T)], [(0, T)]]
-FIRST_CAST_SPLIT = 576
+ROW_LOADS = [[(0, 704), (704, T)], [(0, T // 2), (T // 2, T)], [(0, T)], [(0, T)]]
+FIRST_CAST_SPLIT = 704
 LAST_CAST_SPLIT = 128
 EARLY_SPLIT = 448
 EARLY_VECTOR, EARLY_SCALAR = [(0, EARLY_SPLIT)], [(EARLY_SPLIT, ENTRIES)]
@@ -114,9 +114,7 @@ def tile_picked_hash_lin_relu_sub_l_kernel(tc, xT, w_words, w_scales, b, offs, o
                     nc.vector.tensor_scalar(res[:, m, :], acc[:], bias[:, m : m + 1], 0.0, ADD, MAX)
                 else:
                     nc.scalar.activation(res[:, m, :], acc[:], RELU, bias=bias[:, m : m + 1])
-                if c == CHUNKS - 1:
-                    nc.sync.dma_start(out_rows[:, m, v0:v1], res[:, m, :])
             if c == 1:
                 nc.sync.dma_start(out_rows[:, :, :v1], first_two[:])
-            elif c == 2:
+            elif c >= 2:
                 nc.sync.dma_start(out_rows[:, :, v0:v1], res)

@@ -14,7 +14,6 @@ U8 = mybir.dt.uint8
 FP8X4 = mybir.dt.float8_e4m3fn_x4
 ADD = mybir.AluOpType.add
 MAX = mybir.AluOpType.max
-MULT = mybir.AluOpType.mult
 RELU = mybir.ActivationFunctionType.Relu
 COPY = mybir.ActivationFunctionType.Copy
 
@@ -24,20 +23,9 @@ STRIPE = 16
 ENTRIES = D * V
 CHUNK = 128
 CHUNKS = V // CHUNK
-
-ROW_LOADS = [[(0, 704), (704, T)], [(0, T // 2), (T // 2, T)], [(0, T)], [(0, T)]]
-FIRST_CAST_SPLIT = 704
-LAST_CAST_SPLIT = 128
-EARLY_SPLIT = 448
-EARLY_VECTOR, EARLY_SCALAR = [(0, EARLY_SPLIT)], [(EARLY_SPLIT, ENTRIES)]
-LATE_SPLIT = V // 2 + 32
-LATE_VECTOR = [(0, LATE_SPLIT), (V, V + V // 2)]
-LATE_SCALAR = [(LATE_SPLIT, V), (V + V // 2, ENTRIES)]
-LAST_SCALAR = [(LATE_SPLIT, V), (V + 2 * CHUNK, V + 3 * CHUNK), (V + 3 * CHUNK, ENTRIES)]
-LAST_VECTOR = [(0, LATE_SPLIT), (V, V + CHUNK), (V + CHUNK, V + 2 * CHUNK)]
-VECTOR_PIECES = [EARLY_VECTOR, EARLY_VECTOR, LATE_VECTOR, LAST_VECTOR]
-SCALAR_PIECES = [EARLY_SCALAR, EARLY_SCALAR, LATE_SCALAR, LAST_SCALAR]
-VECTOR_EPILOGUES = [(CHUNKS - 2, 1), (CHUNKS - 1, 1)]
+VECTOR_PIECES = [[(0, V)]] * (ROWS - 1) + [[(0, 256)]]
+SCALAR_PIECES = [[(V, ENTRIES)]] * (ROWS - 1) + [[(V, V + 256), (256, V), (V + 256, V + 384), (V + 384, ENTRIES)]]
+VECTOR_EPILOGUES = [(CHUNKS - 1, 1)]
 
 
 def tile_picked_hash_lin_relu_sub_l_kernel(tc, xT, w_words, w_scales, b, offs, out):
@@ -50,16 +38,18 @@ def tile_picked_hash_lin_relu_sub_l_kernel(tc, xT, w_words, w_scales, b, offs, o
         w_codes = keep.tile([P, N], U32, name="w_codes", align_bytes=64)
         w_plane = keep.tile([P, N], U8, name="w_plane", align_bytes=64)
         bias = keep.tile([P, N // P], F32, name="bias")
-        raw = [keep.tile([P, T], F32, name=f"raw{t}", tag="late" if t == 1 else f"raw{t}") for t in range(ROWS)]
-        cast = [keep.tile([P, T], BF16, name=f"cast{t}") for t in range(ROWS - 1)]
-        picked = keep.tile([P, 2, ENTRIES, 2], BF16, name="picked")
+        raw = [keep.tile([P, T], F32, name=f"raw{t}") for t in range(ROWS)]
+        picked = keep.tile([P, ROWS, ENTRIES], BF16, name="picked")
 
         nc.gpsimd.memset(w_plane[:].bitcast(I32), 0)
 
+        idle = keep.tile([P, 2], F32, name="idle")
+        nc.gpsimd.memset(idle[:, 0:1], 0.0)
+        nc.scalar.activation(idle[:, 1:2], idle[:, 0:1], COPY)
+
         x_rows = xT.rearrange("(p j) c -> p j c", j=ROWS)
         for t in range(ROWS):
-            for c0, c1 in ROW_LOADS[t]:
-                nc.sync.dma_start(raw[t][:, c0:c1], x_rows[:, t, c0:c1])
+            nc.sync.dma_start(raw[t][:], x_rows[:, t, :])
             if t == 0:
                 nc.sync.dma_start(offsets[:], offs)
         nc.sync.dma_start(w_codes[:].bitcast(I32), w_words[0].rearrange("p n t -> p (n t)").bitcast(I32))
@@ -71,41 +61,22 @@ def tile_picked_hash_lin_relu_sub_l_kernel(tc, xT, w_words, w_scales, b, offs, o
         def list_columns(j0, j1):
             return offsets[:, j0 // STRIPE : j1 // STRIPE]
 
-        def gpsimd_cast(t, c0, c1):
-            nc.gpsimd.tensor_scalar(cast[t][:, c0:c1], raw[t][:, c0:c1], 1.0, 0.0, MULT, ADD)
-
-        nc.scalar.copy(cast[0][:, :FIRST_CAST_SPLIT], raw[0][:, :FIRST_CAST_SPLIT])
-        gpsimd_cast(0, FIRST_CAST_SPLIT, T)
         for t in range(ROWS):
-            if t == 2:
-                cast.append(keep.tile([P, T], BF16, name="cast_last", tag="late"))
-                nc.scalar.copy(cast[3][:, :LAST_CAST_SPLIT], raw[3][:, :LAST_CAST_SPLIT])
-            if t == 3:
-                gpsimd_cast(t, LAST_CAST_SPLIT, T)
-            elif t > 0:
-                for c0, c1 in ROW_LOADS[t]:
-                    gpsimd_cast(t, c0, c1)
             for j0, j1 in VECTOR_PIECES[t]:
-                nc.vector.tensor_copy(picked[:, t // 2, j0:j1, t % 2], raw[t][:].indirect(list_columns(j0, j1)))
+                nc.vector.tensor_copy(picked[:, t, j0:j1], raw[t][:].indirect(list_columns(j0, j1)))
             for j0, j1 in SCALAR_PIECES[t]:
-                nc.scalar.activation(picked[:, t // 2, j0:j1, t % 2], cast[t][:].indirect(list_columns(j0, j1)), COPY)
+                nc.scalar.activation(picked[:, t, j0:j1], raw[t][:].indirect(list_columns(j0, j1)), COPY)
 
         out_rows = out.rearrange("(m p) v -> p m v", p=P)
         for c in range(CHUNKS):
             v0, v1 = c * CHUNK, (c + 1) * CHUNK
-            sums = keep.tile([P, CHUNK, 2, 2], BF16, name=f"sums{c}", align_bytes=64)
+            woven = keep.tile([P, CHUNK, ROWS], BF16, name=f"woven{c}", align_bytes=64)
             x_codes = keep.tile([P, CHUNK], U32, name=f"x_codes{c}", align_bytes=64)
             x_plane = keep.tile([P, CHUNK], U8, name=f"x_plane{c}", align_bytes=64)
-            step = CHUNK // 2 if c == CHUNKS - 1 else CHUNK
-            parts = [(s0, s0 + step) for s0 in range(0, CHUNK, step)]
-            for s0, s1 in parts:
-                a0, a1 = [picked[:, :, d * V + v0 + s0 : d * V + v0 + s1, :].rearrange("p h v e -> p v h e") for d in range(D)]
-                nc.vector.tensor_tensor(sums[:, s0:s1], a0, a1, ADD)
-            for s0, s1 in parts:
-                nc.vector.quantize_mx(x_codes[:, s0:s1].bitcast(FP8X4), x_plane[:, s0:s1], sums[:, s0:s1].rearrange("p v h e -> p (v h e)"))
-            if c == 0:
-                first_two = keep.tile([P, N // P, 2 * CHUNK], F32, name="first_two", tag="late")
-            res = first_two[:, :, v0:v1] if c < 2 else keep.tile([P, N // P, CHUNK], F32, name=f"res{c}")[:]
+            a0, a1 = [picked[:, :, d * V + v0 : d * V + v1].rearrange("p t (c i) -> p c t i", i=4) for d in range(D)]
+            nc.vector.tensor_tensor(woven[:].rearrange("p (c i) t -> p c t i", i=4), a0, a1, ADD)
+            nc.vector.quantize_mx(x_codes[:].bitcast(FP8X4), x_plane[:], woven[:].rearrange("p v t -> p (v t)"))
+            res = keep.tile([P, N // P, CHUNK], F32, name=f"res{c}")
             for m in range(N // P):
                 cols = slice(m * P, (m + 1) * P)
                 acc = psum.tile([P, CHUNK], F32, name=f"acc{c}_{m}")
@@ -114,7 +85,4 @@ def tile_picked_hash_lin_relu_sub_l_kernel(tc, xT, w_words, w_scales, b, offs, o
                     nc.vector.tensor_scalar(res[:, m, :], acc[:], bias[:, m : m + 1], 0.0, ADD, MAX)
                 else:
                     nc.scalar.activation(res[:, m, :], acc[:], RELU, bias=bias[:, m : m + 1])
-            if c == 1:
-                nc.sync.dma_start(out_rows[:, :, :v1], first_two[:])
-            elif c >= 2:
-                nc.sync.dma_start(out_rows[:, :, v0:v1], res)
+            nc.sync.dma_start(out_rows[:, :, v0:v1], res[:])

@@ -14,6 +14,7 @@ U8 = mybir.dt.uint8
 FP8X4 = mybir.dt.float8_e4m3fn_x4
 ADD = mybir.AluOpType.add
 MAX = mybir.AluOpType.max
+MULT = mybir.AluOpType.mult
 RELU = mybir.ActivationFunctionType.Relu
 COPY = mybir.ActivationFunctionType.Copy
 
@@ -23,9 +24,13 @@ STRIPE = 16
 ENTRIES = D * V
 CHUNK = 128
 CHUNKS = V // CHUNK
-VECTOR_PIECES = [[(0, V)]] * (ROWS - 1) + [[(0, 256)]]
-SCALAR_PIECES = [[(V, ENTRIES)]] * (ROWS - 1) + [[(V, V + 256), (256, V), (V + 256, V + 384), (V + 384, ENTRIES)]]
-VECTOR_EPILOGUES = [(CHUNKS - 1, 1)]
+
+LOAD_ORDER = [1, 3, 0, 2]
+ROW_LOADS = {1: [(0, T)], 3: [(0, T)], 0: [(0, T // 2), (T // 2, T)], 2: [(0, T)]}
+LATE_SPLIT = V // 2 + 32
+VECTOR_PIECES = {1: [(672, ENTRIES)], 3: [(0, 320)], 0: [(0, 448)], 2: [(0, LATE_SPLIT), (V, V + CHUNK), (V + CHUNK, V + 2 * CHUNK)]}
+SCALAR_PIECES = {1: [(0, 672)], 3: [(320, ENTRIES)], 0: [(448, ENTRIES)], 2: [(LATE_SPLIT, V), (V + 2 * CHUNK, V + 3 * CHUNK), (V + 3 * CHUNK, ENTRIES)]}
+VECTOR_EPILOGUES = [(CHUNKS - 2, 1), (CHUNKS - 1, 1)]
 
 
 def tile_picked_hash_lin_relu_sub_l_kernel(tc, xT, w_words, w_scales, b, offs, out):
@@ -39,7 +44,9 @@ def tile_picked_hash_lin_relu_sub_l_kernel(tc, xT, w_words, w_scales, b, offs, o
         w_plane = keep.tile([P, N], U8, name="w_plane", align_bytes=64)
         bias = keep.tile([P, N // P], F32, name="bias")
         raw = [keep.tile([P, T], F32, name=f"raw{t}") for t in range(ROWS)]
-        picked = keep.tile([P, ROWS, ENTRIES], BF16, name="picked")
+        cast = {t: keep.tile([P, T], BF16, name=f"cast{t}", tag="late" if t == 2 else f"cast{t}") for t in (0, 2)}
+        words = keep.tile([P, 2 * ENTRIES], F32, name="words")
+        halves = words[:].bitcast(BF16).rearrange("p (h j e) -> p h j e", h=2, e=2)
 
         nc.gpsimd.memset(w_plane[:].bitcast(I32), 0)
 
@@ -48,9 +55,10 @@ def tile_picked_hash_lin_relu_sub_l_kernel(tc, xT, w_words, w_scales, b, offs, o
         nc.scalar.activation(idle[:, 1:2], idle[:, 0:1], COPY)
 
         x_rows = xT.rearrange("(p j) c -> p j c", j=ROWS)
-        for t in range(ROWS):
-            nc.sync.dma_start(raw[t][:], x_rows[:, t, :])
-            if t == 0:
+        for t in LOAD_ORDER:
+            for c0, c1 in ROW_LOADS[t]:
+                nc.sync.dma_start(raw[t][:, c0:c1], x_rows[:, t, c0:c1])
+            if t == LOAD_ORDER[0]:
                 nc.sync.dma_start(offsets[:], offs)
         nc.sync.dma_start(w_codes[:].bitcast(I32), w_words[0].rearrange("p n t -> p (n t)").bitcast(I32))
         for q in range(4):
@@ -61,22 +69,34 @@ def tile_picked_hash_lin_relu_sub_l_kernel(tc, xT, w_words, w_scales, b, offs, o
         def list_columns(j0, j1):
             return offsets[:, j0 // STRIPE : j1 // STRIPE]
 
-        for t in range(ROWS):
+        def places(t, j0, j1):
+            if t % 2:
+                return words[:, t // 2 * ENTRIES + j0 : t // 2 * ENTRIES + j1]
+            return halves[:, t // 2, j0:j1, 0]
+
+        for t in LOAD_ORDER:
+            if t in cast:
+                for c0, c1 in ROW_LOADS[t]:
+                    nc.gpsimd.tensor_scalar(cast[t][:, c0:c1], raw[t][:, c0:c1], 1.0, 0.0, MULT, ADD)
             for j0, j1 in VECTOR_PIECES[t]:
-                nc.vector.tensor_copy(picked[:, t, j0:j1], raw[t][:].indirect(list_columns(j0, j1)))
+                nc.vector.tensor_copy(places(t, j0, j1), raw[t][:].indirect(list_columns(j0, j1)))
             for j0, j1 in SCALAR_PIECES[t]:
-                nc.scalar.activation(picked[:, t, j0:j1], raw[t][:].indirect(list_columns(j0, j1)), COPY)
+                nc.scalar.activation(places(t, j0, j1), cast.get(t, raw[t])[:].indirect(list_columns(j0, j1)), COPY)
 
         out_rows = out.rearrange("(m p) v -> p m v", p=P)
         for c in range(CHUNKS):
             v0, v1 = c * CHUNK, (c + 1) * CHUNK
-            woven = keep.tile([P, CHUNK, ROWS], BF16, name=f"woven{c}", align_bytes=64)
+            sums = keep.tile([P, CHUNK, 2, 2], BF16, name=f"sums{c}", align_bytes=64)
             x_codes = keep.tile([P, CHUNK], U32, name=f"x_codes{c}", align_bytes=64)
             x_plane = keep.tile([P, CHUNK], U8, name=f"x_plane{c}", align_bytes=64)
-            a0, a1 = [picked[:, :, d * V + v0 : d * V + v1].rearrange("p t (c i) -> p c t i", i=4) for d in range(D)]
-            nc.vector.tensor_tensor(woven[:].rearrange("p (c i) t -> p c t i", i=4), a0, a1, ADD)
-            nc.vector.quantize_mx(x_codes[:].bitcast(FP8X4), x_plane[:], woven[:].rearrange("p v t -> p (v t)"))
-            res = keep.tile([P, N // P, CHUNK], F32, name=f"res{c}")
+            step = CHUNK // 2 if c == CHUNKS - 1 else CHUNK
+            parts = [(s0, s0 + step) for s0 in range(0, CHUNK, step)]
+            for s0, s1 in parts:
+                a0, a1 = [halves[:, :, d * V + v0 + s0 : d * V + v0 + s1, :].rearrange("p h v e -> p v h e") for d in range(D)]
+                nc.vector.tensor_tensor(sums[:, s0:s1], a0, a1, ADD)
+            for s0, s1 in parts:
+                nc.vector.quantize_mx(x_codes[:, s0:s1].bitcast(FP8X4), x_plane[:, s0:s1], sums[:, s0:s1].rearrange("p v h e -> p (v h e)"))
+            res = keep.tile([P, N // P, CHUNK], F32, name=f"res{c}", tag="late" if c == 0 else f"res{c}")
             for m in range(N // P):
                 cols = slice(m * P, (m + 1) * P)
                 acc = psum.tile([P, CHUNK], F32, name=f"acc{c}_{m}")

@@ -26,10 +26,10 @@ CHUNK = 128
 CHUNKS = V // CHUNK
 
 LOAD_ORDER = [1, 3, 0, 2]
-ROW_LOADS = {1: [(0, T)], 3: [(0, T)], 0: [(0, T // 2), (T // 2, T)], 2: [(0, T)]}
+ROW_LOADS = {1: [(0, T)], 3: [(0, T)], 0: [(0, 384), (384, T)], 2: [(0, T)]}
 LATE_SPLIT = V // 2 + 32
-VECTOR_PIECES = {1: [(672, ENTRIES)], 3: [(0, 320)], 0: [(0, 448)], 2: [(0, LATE_SPLIT), (V, V + CHUNK), (V + CHUNK, V + 2 * CHUNK)]}
-SCALAR_PIECES = {1: [(0, 672)], 3: [(320, ENTRIES)], 0: [(448, ENTRIES)], 2: [(LATE_SPLIT, V), (V + 2 * CHUNK, V + 3 * CHUNK), (V + 3 * CHUNK, ENTRIES)]}
+VECTOR_PIECES = {1: [(640, ENTRIES)], 3: [(0, 352)], 0: [(0, 448)], 2: [(0, LATE_SPLIT), (V, V + CHUNK), (V + CHUNK, V + 2 * CHUNK)]}
+SCALAR_PIECES = {1: [(0, 640)], 3: [(352, ENTRIES)], 0: [(448, ENTRIES)], 2: [(LATE_SPLIT, V), (V + 2 * CHUNK, V + 3 * CHUNK), (V + 3 * CHUNK, ENTRIES)]}
 VECTOR_EPILOGUES = [(CHUNKS - 2, 1), (CHUNKS - 1, 1)]
 
 

@@ -27,7 +27,7 @@ CHUNKS = V // CHUNK
 
 LOAD_ORDER = [1, 3, 0, 2]
 ROW_LOADS = {1: [(0, T)], 3: [(0, T)], 0: [(0, 384), (384, T)], 2: [(0, T)]}
-LATE_SPLIT = V // 2 + 32
+LATE_SPLIT = V // 2 + 64
 VECTOR_PIECES = {1: [(640, ENTRIES)], 3: [(0, 352)], 0: [(0, 448)], 2: [(0, LATE_SPLIT), (V, V + CHUNK), (V + CHUNK, V + 2 * CHUNK)]}
 SCALAR_PIECES = {1: [(0, 640)], 3: [(352, ENTRIES)], 0: [(448, ENTRIES)], 2: [(LATE_SPLIT, V), (V + 2 * CHUNK, V + 3 * CHUNK), (V + 3 * CHUNK, ENTRIES)]}
 VECTOR_EPILOGUES = [(CHUNKS - 2, 1), (CHUNKS - 1, 1)]

@@ -14,7 +14,6 @@ U8 = mybir.dt.uint8
 FP8X4 = mybir.dt.float8_e4m3fn_x4
 ADD = mybir.AluOpType.add
 MAX = mybir.AluOpType.max
-MULT = mybir.AluOpType.mult
 RELU = mybir.ActivationFunctionType.Relu
 COPY = mybir.ActivationFunctionType.Copy
 
@@ -27,9 +26,8 @@ CHUNKS = V // CHUNK
 
 LOAD_ORDER = [1, 3, 0, 2]
 ROW_LOADS = {1: [(0, T)], 3: [(0, T)], 0: [(0, 384), (384, T)], 2: [(0, T)]}
-LATE_SPLIT = V // 2 + 64
-VECTOR_PIECES = {1: [(640, ENTRIES)], 3: [(0, 352)], 0: [(0, 448)], 2: [(0, LATE_SPLIT), (V, V + CHUNK), (V + CHUNK, V + 2 * CHUNK)]}
-SCALAR_PIECES = {1: [(0, 640)], 3: [(352, ENTRIES)], 0: [(448, ENTRIES)], 2: [(LATE_SPLIT, V), (V + 2 * CHUNK, V + 3 * CHUNK), (V + 3 * CHUNK, ENTRIES)]}
+VECTOR_PIECES = {1: [(608, ENTRIES)], 3: [(0, 352)], 0: [(0, 448)], 2: [(0, 320), (512, 640), (640, 768)]}
+SCALAR_PIECES = {1: [(0, 608)], 3: [(352, ENTRIES)], 0: [(448, ENTRIES)], 2: [(320, 512), (768, 896), (896, ENTRIES)]}
 VECTOR_EPILOGUES = [(CHUNKS - 2, 1), (CHUNKS - 1, 1)]
 
 
@@ -77,7 +75,7 @@ def tile_picked_hash_lin_relu_sub_l_kernel(tc, xT, w_words, w_scales, b, offs, o
         for t in LOAD_ORDER:
             if t in cast:
                 for c0, c1 in ROW_LOADS[t]:
-                    nc.gpsimd.tensor_scalar(cast[t][:, c0:c1], raw[t][:, c0:c1], 1.0, 0.0, MULT, ADD)
+                    nc.gpsimd.tensor_copy(cast[t][:, c0:c1], raw[t][:, c0:c1])
             for j0, j1 in VECTOR_PIECES[t]:
                 nc.vector.tensor_copy(places(t, j0, j1), raw[t][:].indirect(list_columns(j0, j1)))
             for j0, j1 in SCALAR_PIECES[t]:

@@ -25,9 +25,9 @@ CHUNK = 128
 CHUNKS = V // CHUNK
 
 LOAD_ORDER = [1, 3, 0, 2]
-ROW_LOADS = {1: [(0, T)], 3: [(0, T)], 0: [(0, 384), (384, T)], 2: [(0, T)]}
-VECTOR_PIECES = {1: [(608, ENTRIES)], 3: [(0, 352)], 0: [(0, 448)], 2: [(0, 320), (512, 640), (640, 768)]}
-SCALAR_PIECES = {1: [(0, 608)], 3: [(352, ENTRIES)], 0: [(448, ENTRIES)], 2: [(320, 512), (768, 896), (896, ENTRIES)]}
+ROW_LOADS = {1: [(0, T)], 3: [(0, T)], 0: [(0, 448), (448, T)], 2: [(0, T)]}
+VECTOR_PIECES = {1: [(608, ENTRIES)], 3: [(0, 384)], 0: [(0, 416)], 2: [(0, 352), (512, 640), (640, 768)]}
+SCALAR_PIECES = {1: [(0, 608)], 3: [(384, ENTRIES)], 0: [(416, ENTRIES)], 2: [(352, 512), (768, 896), (896, ENTRIES)]}
 VECTOR_EPILOGUES = [(CHUNKS - 2, 1), (CHUNKS - 1, 1)]
 
 

from contextlib import ExitStack

import concourse.mybir as mybir

K, T, D, V, N = 512, 1024, 2, 512, 256
FLOPS = 2 * K * V * N

F32 = mybir.dt.float32
BF16 = mybir.dt.bfloat16
U32 = mybir.dt.uint32
I32 = mybir.dt.int32
U16 = mybir.dt.uint16
U8 = mybir.dt.uint8
FP8X4 = mybir.dt.float8_e4m3fn_x4
ADD = mybir.AluOpType.add
MAX = mybir.AluOpType.max
RELU = mybir.ActivationFunctionType.Relu
COPY = mybir.ActivationFunctionType.Copy

P = 128
ROWS = 4
STRIPE = 16
ENTRIES = D * V
CHUNK = 128
CHUNKS = V // CHUNK

LOAD_ORDER = [1, 3, 0, 2]
ROW_LOADS = {1: [(0, T)], 3: [(0, T)], 0: [(0, 448), (448, T)], 2: [(0, T)]}
VECTOR_PIECES = {1: [(608, ENTRIES)], 3: [(0, 384)], 0: [(0, 416)], 2: [(0, 352), (512, 640), (640, 768)]}
SCALAR_PIECES = {1: [(0, 608)], 3: [(384, ENTRIES)], 0: [(416, ENTRIES)], 2: [(352, 512), (768, 896), (896, ENTRIES)]}
VECTOR_EPILOGUES = [(CHUNKS - 2, 1), (CHUNKS - 1, 1)]


def tile_picked_hash_lin_relu_sub_l_kernel(tc, xT, w_words, w_scales, b, offs, out):
    nc = tc.nc
    with ExitStack() as ctx:
        keep = ctx.enter_context(tc.tile_pool(name="keep", bufs=1))
        psum = ctx.enter_context(tc.psum_pool(name="psum", bufs=1))

        offsets = keep.tile([P, ENTRIES // STRIPE], U16, name="offsets")
        w_codes = keep.tile([P, N], U32, name="w_codes", align_bytes=64)
        w_plane = keep.tile([P, N], U8, name="w_plane", align_bytes=64)
        bias = keep.tile([P, N // P], F32, name="bias")
        raw = [keep.tile([P, T], F32, name=f"raw{t}") for t in range(ROWS)]
        cast = {t: keep.tile([P, T], BF16, name=f"cast{t}", tag="late" if t == 2 else f"cast{t}") for t in (0, 2)}
        words = keep.tile([P, 2 * ENTRIES], F32, name="words")
        halves = words[:].bitcast(BF16).rearrange("p (h j e) -> p h j e", h=2, e=2)

        nc.gpsimd.memset(w_plane[:].bitcast(I32), 0)

        idle = keep.tile([P, 2], F32, name="idle")
        nc.gpsimd.memset(idle[:, 0:1], 0.0)
        nc.scalar.activation(idle[:, 1:2], idle[:, 0:1], COPY)

        x_rows = xT.rearrange("(p j) c -> p j c", j=ROWS)
        for t in LOAD_ORDER:
            for c0, c1 in ROW_LOADS[t]:
                nc.sync.dma_start(raw[t][:, c0:c1], x_rows[:, t, c0:c1])
            if t == LOAD_ORDER[0]:
                nc.sync.dma_start(offsets[:], offs)
        nc.sync.dma_start(w_codes[:].bitcast(I32), w_words[0].rearrange("p n t -> p (n t)").bitcast(I32))
        for q in range(4):
            nc.sync.dma_start(w_plane[32 * q : 32 * q + 4, :].bitcast(I32), w_scales[0, 4 * q : 4 * q + 4, :].bitcast(I32))
        with nc.allow_non_contiguous_dma(reason="one bias value for each partition and half"):
            nc.sync.dma_start(bias[:], b.rearrange("(c p) o -> p (c o)", p=P))

        def list_columns(j0, j1):
            return offsets[:, j0 // STRIPE : j1 // STRIPE]

        def places(t, j0, j1):
            if t % 2:
                return words[:, t // 2 * ENTRIES + j0 : t // 2 * ENTRIES + j1]
            return halves[:, t // 2, j0:j1, 0]

        for t in LOAD_ORDER:
            if t in cast:
                for c0, c1 in ROW_LOADS[t]:
                    nc.gpsimd.tensor_copy(cast[t][:, c0:c1], raw[t][:, c0:c1])
            for j0, j1 in VECTOR_PIECES[t]:
                nc.vector.tensor_copy(places(t, j0, j1), raw[t][:].indirect(list_columns(j0, j1)))
            for j0, j1 in SCALAR_PIECES[t]:
                nc.scalar.activation(places(t, j0, j1), cast.get(t, raw[t])[:].indirect(list_columns(j0, j1)), COPY)

        out_rows = out.rearrange("(m p) v -> p m v", p=P)
        for c in range(CHUNKS):
            v0, v1 = c * CHUNK, (c + 1) * CHUNK
            sums = keep.tile([P, CHUNK, 2, 2], BF16, name=f"sums{c}", align_bytes=64)
            x_codes = keep.tile([P, CHUNK], U32, name=f"x_codes{c}", align_bytes=64)
            x_plane = keep.tile([P, CHUNK], U8, name=f"x_plane{c}", align_bytes=64)
            step = CHUNK // 2 if c == CHUNKS - 1 else CHUNK
            parts = [(s0, s0 + step) for s0 in range(0, CHUNK, step)]
            for s0, s1 in parts:
                a0, a1 = [halves[:, :, d * V + v0 + s0 : d * V + v0 + s1, :].rearrange("p h v e -> p v h e") for d in range(D)]
                nc.vector.tensor_tensor(sums[:, s0:s1], a0, a1, ADD)
            for s0, s1 in parts:
                nc.vector.quantize_mx(x_codes[:, s0:s1].bitcast(FP8X4), x_plane[:, s0:s1], sums[:, s0:s1].rearrange("p v h e -> p (v h e)"))
            res = keep.tile([P, N // P, CHUNK], F32, name=f"res{c}", tag="late" if c == 0 else f"res{c}")
            for m in range(N // P):
                cols = slice(m * P, (m + 1) * P)
                acc = psum.tile([P, CHUNK], F32, name=f"acc{c}_{m}")
                nc.tensor.matmul_mx(acc[:], w_codes[:, cols].bitcast(FP8X4), w_plane[:, cols], x_codes[:].bitcast(FP8X4), x_plane[:], start=True, stop=True)
                if (c, m) in VECTOR_EPILOGUES:
                    nc.vector.tensor_scalar(res[:, m, :], acc[:], bias[:, m : m + 1], 0.0, ADD, MAX)
                else:
                    nc.scalar.activation(res[:, m, :], acc[:], RELU, bias=bias[:, m : m + 1])
            nc.sync.dma_start(out_rows[:, :, v0:v1], res[:])
